import numpy as np, ml_dtypes
CORES = [15,47,79,175,207]
N = 5
import mx_ref
NC, G = 128, 2
C = np.float32(0.01923)
BF = ml_dtypes.bfloat16
def cut(t, i, w=512):
    return t[:, w * i:w * i + w]
def tile(rs):
    return np.stack(rs, axis=2).reshape(128, -1).astype(BF)
def layer(w, X):
    out = []
    for i in range(G):
        for t in range(len(X)):
            p = mx_ref.matmul(mx_ref.quantize(cut(w, len(X) * i + t)), X[t])
            z = p if t == 0 else z + p
        out.append(z)
    return out
def act(Z):
    return [np.maximum(s * z, 0) * C for z in Z for s in (1, -1)]
def setup_inputs(rng):
    def f(*shape):
        return mx_ref.flush((rng.standard_normal(shape, dtype=np.float32) * np.exp2(rng.integers(-2, 3, shape[:-1] + (1,)))).astype(BF))
    return {"x": f(N, 128, N * 4 * NC), "w1": f(N, 128, G * 512), "w2": f(N, 128, 512)}
def setup_inputs_blocks(rng):
    d = setup_inputs(rng)
    for k in ("x", "w1", "w2"): d[k] = mx_ref.spread(d[k], rng, 4)
    return d
def setup_inputs_wide(rng):
    d = setup_inputs(rng)
    for k in ("x", "w1", "w2"): d[k] = mx_ref.flush((d[k].astype(np.float32) * np.exp2(rng.integers(-6, 7, (N, 1, 1))).astype(np.float32)).astype(BF))
    return d
def reference(x, w1, w2, own=None):
    h = np.zeros((N, 128, 4 * NC), BF)
    for c in range(N):
        for j in range(N):
            P = layer(w1[j], [mx_ref.quantize(cut(x[j], c, 4 * NC))])
            Z = P if j == 0 else [z + p for z, p in zip(Z, P)]
        h[c] = tile(act(Z))
    use = h if own is None else own["h"]
    H = [mx_ref.quantize(use[j]) for j in range(N)]
    y = np.zeros((N, 128, N * NC), np.float32)
    for r in range(N):
        qw = mx_ref.quantize(w2[r])
        for j in range(N):
            y[r][:, NC * j:NC * j + NC] = mx_ref.matmul(qw, H[j])
    return {"h": h, "y": y}

@@ -1,0 +1,177 @@
+from concourse.bass import DstId, RemoteDMATransfer
+from concourse.mybir import dt, AluOpType, ActivationFunctionType
+
+N = 5
+NC = 128
+TW = 4 * NC
+PW = 2 * NC
+CS = 0.01923
+
+SCRATCH = {
+    "xs": ("sbuf", [128, N * TW], "bfloat16"),
+    "w1s": ("sbuf", [128, 2 * TW], "bfloat16"),
+    "w2s": ("sbuf", [128, TW], "bfloat16"),
+    "xq": ("sbuf", [128, N * NC], "float8_e4m3fn_x4"),
+    "xp": ("sbuf", [128, N * NC], "uint8"),
+    "w1q": ("sbuf", [128, 2 * NC], "float8_e4m3fn_x4"),
+    "w1p": ("sbuf", [128, 2 * NC], "uint8"),
+    "w2q": ("sbuf", [128, NC], "float8_e4m3fn_x4"),
+    "w2p": ("sbuf", [128, NC], "uint8"),
+    "out1": ("sbuf", [128, 4 * PW], "float32"),
+    "land": ("sbuf", [128, 4 * PW], "float32"),
+    "acc": ("sbuf", [128, PW], "float32"),
+    "ht": ("sbuf", [128, TW], "bfloat16"),
+    "hq": ("sbuf", [128, NC], "float8_e4m3fn_x4"),
+    "hp": ("sbuf", [128, NC], "uint8"),
+    "gq": ("sbuf", [128, 4 * NC], "float8_e4m3fn_x4"),
+    "gp": ("sbuf", [128, 4 * NC], "uint8"),
+    "ys": ("sbuf", [128, N * NC], "float32"),
+}
+for _b in range(8):
+    SCRATCH["ps%d" % _b] = ("psum", [128, 512], "float32")
+
+SEMAPHORES = (
+    ["ldw1", "ldw2", "qw1", "qw2", "left1", "left2", "hdone", "qh", "st"]
+    + ["ldx%d" % k for k in range(N)] + ["qx%d" % k for k in range(N)]
+    + ["mma%d" % k for k in range(N)] + ["mmb%d" % k for k in range(N)]
+    + ["cp%d" % k for k in range(1, N)] + ["ad%d" % k for k in range(1, N)]
+    + ["pf%d" % j for j in range(N)]
+    + ["hf%d" % j for j in range(N)]
+    + ["ym%d" % k for k in range(N)] + ["yc%d" % k for k in range(N)]
+)
+
+
+def rank_program(g, core, T, topo):
+    r = T.rank_of(core)
+    if r is None:
+        return
+    S = T.sem
+    vec, ten, act, syn = g.vector, g.tensor, g.scalar, g.sync
+    ahead = [(r + k) % N for k in range(N)]
+    behind = [(r - k) % N for k in range(N)]
+    order = [1, 2, 3, 4, 0]
+    add = AluOpType.add
+
+    dest = [T.cores[c] for c in ahead]
+    where = [None] + [topo.addr(dest[k], core) for k in range(1, N)]
+    masks = [None] + [topo.mask(core, dest[k]) for k in range(1, N)]
+    common = masks[1] & masks[2] & masks[3] & masks[4]
+    lanes = [0] + [bin(masks[k]).count("1") for k in range(1, N)]
+    lanes_common = bin(common).count("1")
+
+    def lanes_of(j, every):
+        m = topo.mask(T.cores[j], core)
+        if every:
+            for c in range(N):
+                if c != j:
+                    m &= topo.mask(T.cores[j], T.cores[c])
+        return bin(m).count("1")
+
+    def bank1(k, i):
+        return T["ps%d" % (2 * (k - 1) + i if k else i)]
+
+    def bank2(k):
+        return T["ps%d" % (2 + k)]
+
+    def load_x(queue, k):
+        c = ahead[k]
+        queue.dma_start(T.xs[:, TW * c:TW * (c + 1)], T.x[:, TW * c:TW * (c + 1)]).then_inc(S["ldx%d" % k], 16)
+
+    syn.dma_start(T.w1s[:], T.w1[:]).then_inc(S.ldw1, 16)
+    load_x(act, 1)
+    load_x(syn, 2)
+    load_x(act, 3)
+    load_x(syn, 4)
+    load_x(act, 0)
+
+    vec.wait_ge(S.ldw1, 16)
+    vec.quantize_mx(T.w1q[:], T.w1p[:], T.w1s[:]).then_inc(S.qw1, 1)
+    ten.wait_ge(S.qw1, 1)
+    for k in order:
+        c = ahead[k]
+        vec.wait_ge(S["ldx%d" % k], 16)
+        vec.quantize_mx(T.xq[:, NC * c:NC * (c + 1)], T.xp[:, NC * c:NC * (c + 1)],
+                        T.xs[:, TW * c:TW * (c + 1)]).then_inc(S["qx%d" % k], 1)
+        ten.wait_ge(S["qx%d" % k], 1)
+        if k == 0:
+            ten.wait_ge(S.cp1, 2)
+        for i, name in ((0, "mma%d"), (1, "mmb%d")):
+            ten.matmul_mx(bank1(k, i)[:, 0:NC], T.w1q[:, NC * i:NC * (i + 1)], T.w1p[:, NC * i:NC * (i + 1)],
+                          T.xq[:, NC * c:NC * (c + 1)], T.xp[:, NC * c:NC * (c + 1)], True, True).then_inc(S[name % k], 1)
+        if k == 0:
+            continue
+        lo, hi = PW * (k - 1), PW * k
+        vec.wait_ge(S["mma%d" % k], 1)
+        vec.tensor_copy(T.out1[:, lo:hi:2], bank1(k, 0)[:, 0:NC]).then_inc(S["cp%d" % k], 1)
+        act.wait_ge(S["mmb%d" % k], 1)
+        act.activation(T.out1[:, lo + 1:hi:2], bank1(k, 1)[:, 0:NC], ActivationFunctionType.Copy).then_inc(S["cp%d" % k], 1)
+        g.wait_ge(S["cp%d" % k], 2)
+        g.remote_dma(out_ap=T.land[:, lo:hi], in_ap=T.out1[:, lo:hi], remote_sem=S["pf%d" % r], local_sem=S.left1,
+                     pid=where[k][1], routing_id=where[k][0], dma_engine_mask=masks[k])
+    left1 = sum(lanes)
+
+    syn.wait_ge(S.left1, left1)
+    syn.dma_start(T.w2s[:], T.w2[:]).then_inc(S.ldw2, 16)
+
+    vec.wait_ge(S["pf%d" % behind[1]], lanes_of(behind[1], False))
+    vec.wait_ge(S.mma0, 1)
+    vec.wait_ge(S.mmb0, 1)
+    vec.tensor_tensor(T.acc[:, 0:PW:2], T.land[:, 0:PW:2], bank1(0, 0)[:, 0:NC], add).then_inc(S.ad1, 1)
+    vec.tensor_tensor(T.acc[:, 1:PW:2], T.land[:, 1:PW:2], bank1(0, 1)[:, 0:NC], add).then_inc(S.ad1, 1)
+    for k in (2, 3, 4):
+        vec.wait_ge(S["ad%d" % (k - 1)], 2 if k == 2 else 1)
+        vec.wait_ge(S["pf%d" % behind[k]], lanes_of(behind[k], False))
+        vec.tensor_tensor(T.acc[:], T.acc[:], T.land[:, PW * (k - 1):PW * k], add).then_inc(S["ad%d" % k], 1)
+
+    vec.wait_ge(S.ad4, 1)
+    vec.tensor_scalar(T.ht[:, 0:TW:2], T.acc[:], 0.0, CS, AluOpType.max, AluOpType.mult).then_inc(S.hdone, 1)
+    act.wait_ge(S.ad4, 1)
+    act.activation(T.ht[:, 1:TW:2], T.acc[:], ActivationFunctionType.Relu, scale=-CS).then_inc(S.hdone, 1)
+    vec.wait_ge(S.hdone, 2)
+    vec.quantize_mx(T.hq[:], T.hp[:], T.ht[:]).then_inc(S.qh, 1)
+    vec.wait_ge(S.ldw2, 16)
+    vec.quantize_mx(T.w2q[:], T.w2p[:], T.w2s[:]).then_inc(S.qw2, 1)
+
+    g.wait_ge(S.qh, 1)
+    g.remote_dma_fused([RemoteDMATransfer(
+        dst_ids=[DstId(rid=where[k][0], pnc=where[k][1]) for k in range(1, N)], dma_engine_mask=common,
+        remote_sem=S["hf%d" % r], srcs=[T.hp[:]], dsts=[T.gp[:, NC * (k - 1):NC * k] for k in range(1, N)])],
+        local_sem=S.left2)
+    for k in range(1, N):
+        g.remote_dma(out_ap=T.gq[:, NC * (k - 1):NC * k].bitcast(dt.uint8), in_ap=T.hq[:].bitcast(dt.uint8),
+                     remote_sem=S["hf%d" % r], local_sem=S.left2,
+                     pid=where[k][1], routing_id=where[k][0], dma_engine_mask=masks[k])
+    left2 = lanes_common + sum(lanes)
+
+    ten.wait_ge(S.qh, 1)
+    ten.wait_ge(S.qw2, 1)
+    for k in range(N):
+        ten.wait_ge(S["cp%d" % ((2 + k) // 2 + 1)], 2)
+        if k == 0:
+            rhs, rhs_scale = T.hq[:], T.hp[:]
+        else:
+            ten.wait_ge(S["hf%d" % behind[k]], lanes_of(behind[k], True) + lanes_of(behind[k], False))
+            rhs, rhs_scale = T.gq[:, NC * (k - 1):NC * k], T.gp[:, NC * (k - 1):NC * k]
+        ten.matmul_mx(bank2(k)[:, 0:NC], T.w2q[:], T.w2p[:], rhs, rhs_scale, True, True).then_inc(S["ym%d" % k], 1)
+        j = behind[k]
+        vec.wait_ge(S["ym%d" % k], 1)
+        vec.tensor_copy(T.ys[:, NC * j:NC * (j + 1)], bank2(k)[:, 0:NC]).then_inc(S["yc%d" % k], 1)
+
+    def store_y(queue, k):
+        j = behind[k]
+        queue.wait_ge(S["yc%d" % k], 1)
+        queue.dma_start(T.y[:, NC * j:NC * (j + 1)], T.ys[:, NC * j:NC * (j + 1)]).then_inc(S.st, 16)
+
+    syn.wait_ge(S.hdone, 2)
+    syn.wait_ge(S.left2, left2)
+    act.wait_ge(S.left2, left2)
+    syn.dma_start(T.h[:], T.ht[:]).then_inc(S.st, 16)
+    store_y(act, 0)
+    store_y(syn, 1)
+    store_y(act, 2)
+    store_y(syn, 3)
+    store_y(act, 4)
+
+    g.wait_ge(S.left1, left1)
+    g.wait_ge(S.left2, left2)
+    g.wait_ge(S.st, 16 * (N + 1))

@@ -2,10 +2,16 @@ from concourse.bass import DstId, RemoteDMATransfer
 from concourse.mybir import dt, AluOpType, ActivationFunctionType
 
 N = 5
+WORLD = 256
 NC = 128
 TW = 4 * NC
 PW = 2 * NC
 CS = 0.01923
+NEAR = (1, 2, 3)
+FAR = 4
+DIRECT = (1, 2)
+RELAYED = (3, 4)
+HAND_ALL = True
 
 SCRATCH = {
     "xs": ("sbuf", [128, N * TW], "bfloat16"),
@@ -17,8 +23,18 @@ SCRATCH = {
     "w1p": ("sbuf", [128, 2 * NC], "uint8"),
     "w2q": ("sbuf", [128, NC], "float8_e4m3fn_x4"),
     "w2p": ("sbuf", [128, NC], "uint8"),
-    "out1": ("sbuf", [128, 4 * PW], "float32"),
-    "land": ("sbuf", [128, 4 * PW], "float32"),
+    "fw1q": ("sbuf", [128, 2 * NC], "float8_e4m3fn_x4"),
+    "fw1p": ("sbuf", [128, 2 * NC], "uint8"),
+    "fxq": ("sbuf", [128, NC], "float8_e4m3fn_x4"),
+    "fxp": ("sbuf", [128, NC], "uint8"),
+    "fq": ("sbuf", [128, NC], "float8_e4m3fn_x4"),
+    "fp": ("sbuf", [128, NC], "uint8"),
+    "rw1q": ("sbuf", [128, 2 * NC], "float8_e4m3fn_x4"),
+    "rw1p": ("sbuf", [128, 2 * NC], "uint8"),
+    "rxq": ("sbuf", [128, NC], "float8_e4m3fn_x4"),
+    "rxp": ("sbuf", [128, NC], "uint8"),
+    "out1": ("sbuf", [128, 3 * PW], "float32"),
+    "land": ("sbuf", [128, 3 * PW], "float32"),
     "acc": ("sbuf", [128, PW], "float32"),
     "ht": ("sbuf", [128, TW], "bfloat16"),
     "hq": ("sbuf", [128, NC], "float8_e4m3fn_x4"),
@@ -31,73 +47,138 @@ for _b in range(8):
     SCRATCH["ps%d" % _b] = ("psum", [128, 512], "float32")
 
 SEMAPHORES = (
-    ["ldw1", "ldw2", "qw1", "qw2", "left1", "left2", "hdone", "qh", "st"]
+    ["ldw1", "ldw2", "qw1", "qw2", "left1", "left2", "hdone", "qh", "st",
+     "r1s", "r1c", "rs", "rc",
+     "cw", "cx", "mz0", "mz1", "ad2", "ad3", "ad4"]
     + ["ldx%d" % k for k in range(N)] + ["qx%d" % k for k in range(N)]
-    + ["mma%d" % k for k in range(N)] + ["mmb%d" % k for k in range(N)]
-    + ["cp%d" % k for k in range(1, N)] + ["ad%d" % k for k in range(1, N)]
+    + ["mma%d" % k for k in NEAR] + ["mmb%d" % k for k in NEAR] + ["cp%d" % k for k in NEAR]
     + ["pf%d" % j for j in range(N)]
     + ["hf%d" % j for j in range(N)]
     + ["ym%d" % k for k in range(N)] + ["yc%d" % k for k in range(N)]
 )
 
 
+def _bits(m):
+    return bin(m).count("1")
+
+
+def _plan(topo, T, j):
+    rc = T.cores[j]
+    others = [T.cores[c] for c in range(N) if c != j]
+    free = [c for c in range(WORLD)
+            if topo.host(c) == topo.host(rc) and topo.chip(c) == topo.chip(rc) and topo.die(c) != topo.die(rc)
+            and T.rank_of(c) is None and all(topo.may_write(c, d) for d in others)]
+    relay = {k: free[n] for n, k in enumerate(RELAYED)}
+    away = topo.mask(rc, others[0])
+    for d in others:
+        away &= topo.mask(rc, d)
+    home = topo.mask(rc, relay[RELAYED[0]])
+    for k in RELAYED:
+        home &= topo.mask(rc, relay[k])
+    stay = home & ~away
+    stay = stay if stay else home
+    return {"relay": relay, "away": away, "home": stay, "hand": home if HAND_ALL else stay}
+
+
+def _relay_program(g, core, T, topo, j, k, plan):
+    S = T.sem
+    u8 = dt.uint8
+
+    def send(dst, out_ap, in_ap, sem):
+        rid, pid = topo.addr(dst, core)
+        g.remote_dma(out_ap=out_ap, in_ap=in_ap, remote_sem=sem, local_sem=S.left2, pid=pid, routing_id=rid,
+                     dma_engine_mask=topo.mask(core, dst))
+        return _bits(topo.mask(core, dst))
+
+    far = T.cores[(j + FAR) % N]
+    if k == RELAYED[0]:
+        sp, sq, dp, dq, sem = T.fw1p, T.fw1q, T.rw1p, T.rw1q, S.cw
+    else:
+        sp, sq, dp, dq, sem = T.fxp, T.fxq, T.rxp, T.rxq, S.cx
+    left = 0
+    g.wait_ge(S.r1s, _bits(plan["home"]))
+    left += send(far, dp[:], sp[:], sem)
+    g.wait_ge(S.r1c, _bits(plan["home"]))
+    left += send(far, dq[:].bitcast(u8), sq[:].bitcast(u8), sem)
+    dst = T.cores[(j + k) % N]
+    g.wait_ge(S.rs, _bits(plan["hand"]))
+    left += send(dst, T.gp[:, NC * (k - 1):NC * k], T.fp[:], S["hf%d" % j])
+    g.wait_ge(S.rc, _bits(plan["hand"]))
+    left += send(dst, T.gq[:, NC * (k - 1):NC * k].bitcast(u8), T.fq[:].bitcast(u8), S["hf%d" % j])
+    g.wait_ge(S.left2, left)
+
+
 def rank_program(g, core, T, topo):
     r = T.rank_of(core)
+    plans = [_plan(topo, T, j) for j in range(N)]
     if r is None:
+        for j in range(N):
+            for k in RELAYED:
+                if plans[j]["relay"][k] == core:
+                    _relay_program(g, core, T, topo, j, k, plans[j])
         return
     S = T.sem
+    u8 = dt.uint8
     vec, ten, act, syn = g.vector, g.tensor, g.scalar, g.sync
     ahead = [(r + k) % N for k in range(N)]
     behind = [(r - k) % N for k in range(N)]
-    order = [1, 2, 3, 4, 0]
     add = AluOpType.add
+    mine = plans[r]
+    home = mine["home"]
 
     dest = [T.cores[c] for c in ahead]
     where = [None] + [topo.addr(dest[k], core) for k in range(1, N)]
     masks = [None] + [topo.mask(core, dest[k]) for k in range(1, N)]
-    common = masks[1] & masks[2] & masks[3] & masks[4]
-    lanes = [0] + [bin(masks[k]).count("1") for k in range(1, N)]
-    lanes_common = bin(common).count("1")
-
-    def lanes_of(j, every):
-        m = topo.mask(T.cores[j], core)
-        if every:
-            for c in range(N):
-                if c != j:
-                    m &= topo.mask(T.cores[j], T.cores[c])
-        return bin(m).count("1")
+    lanes = [0] + [_bits(masks[k]) for k in range(1, N)]
+    hand = {k: topo.addr(mine["relay"][k], core) for k in RELAYED}
 
     def bank1(k, i):
-        return T["ps%d" % (2 * (k - 1) + i if k else i)]
+        return T["ps%d" % (2 * (k - 1) + i if k else 6 + i)]
 
     def bank2(k):
-        return T["ps%d" % (2 + k)]
+        return T["ps%d" % k]
+
+    def xcols(k):
+        c = ahead[k]
+        return NC * c, NC * (c + 1)
 
     def load_x(queue, k):
         c = ahead[k]
         queue.dma_start(T.xs[:, TW * c:TW * (c + 1)], T.x[:, TW * c:TW * (c + 1)]).then_inc(S["ldx%d" % k], 16)
 
     syn.dma_start(T.w1s[:], T.w1[:]).then_inc(S.ldw1, 16)
-    load_x(act, 1)
-    load_x(syn, 2)
-    load_x(act, 3)
-    load_x(syn, 4)
+    load_x(act, FAR)
+    load_x(syn, 1)
+    load_x(act, 2)
+    load_x(syn, 3)
     load_x(act, 0)
 
-    vec.wait_ge(S.ldw1, 16)
-    vec.quantize_mx(T.w1q[:], T.w1p[:], T.w1s[:]).then_inc(S.qw1, 1)
+    def to_relay(k, out_ap, in_ap, sem):
+        g.remote_dma(out_ap=out_ap, in_ap=in_ap, remote_sem=sem, local_sem=S.left1,
+                     pid=hand[k][1], routing_id=hand[k][0], dma_engine_mask=home)
+
     ten.wait_ge(S.qw1, 1)
-    for k in order:
-        c = ahead[k]
+    for k in (FAR,) + NEAR + (0,):
+        lo_x, hi_x = xcols(k)
         vec.wait_ge(S["ldx%d" % k], 16)
-        vec.quantize_mx(T.xq[:, NC * c:NC * (c + 1)], T.xp[:, NC * c:NC * (c + 1)],
-                        T.xs[:, TW * c:TW * (c + 1)]).then_inc(S["qx%d" % k], 1)
+        vec.quantize_mx(T.xq[:, lo_x:hi_x], T.xp[:, lo_x:hi_x],
+                        T.xs[:, 4 * lo_x:4 * hi_x]).then_inc(S["qx%d" % k], 1)
+        if k == FAR:
+            vec.wait_ge(S.ldw1, 16)
+            vec.quantize_mx(T.w1q[:], T.w1p[:], T.w1s[:]).then_inc(S.qw1, 1)
+            g.wait_ge(S["qx%d" % k], 1)
+            to_relay(RELAYED[1], T.fxp[:], T.xp[:, lo_x:hi_x], S.r1s)
+            g.wait_ge(S.qw1, 1)
+            to_relay(RELAYED[0], T.fw1p[:], T.w1p[:], S.r1s)
+            to_relay(RELAYED[0], T.fw1q[:].bitcast(u8), T.w1q[:].bitcast(u8), S.r1c)
+            to_relay(RELAYED[1], T.fxq[:].bitcast(u8), T.xq[:, lo_x:hi_x].bitcast(u8), S.r1c)
+            continue
         ten.wait_ge(S["qx%d" % k], 1)
-        if k == 0:
-            ten.wait_ge(S.cp1, 2)
         for i, name in ((0, "mma%d"), (1, "mmb%d")):
-            ten.matmul_mx(bank1(k, i)[:, 0:NC], T.w1q[:, NC * i:NC * (i + 1)], T.w1p[:, NC * i:NC * (i + 1)],
-                          T.xq[:, NC * c:NC * (c + 1)], T.xp[:, NC * c:NC * (c + 1)], True, True).then_inc(S[name % k], 1)
+            mm = ten.matmul_mx(bank1(k, i)[:, 0:NC], T.w1q[:, NC * i:NC * (i + 1)], T.w1p[:, NC * i:NC * (i + 1)],
+                               T.xq[:, lo_x:hi_x], T.xp[:, lo_x:hi_x], True, k != 0)
+            if k:
+                mm.then_inc(S[name % k], 1)
         if k == 0:
             continue
         lo, hi = PW * (k - 1), PW * k
@@ -108,49 +189,74 @@ def rank_program(g, core, T, topo):
         g.wait_ge(S["cp%d" % k], 2)
         g.remote_dma(out_ap=T.land[:, lo:hi], in_ap=T.out1[:, lo:hi], remote_sem=S["pf%d" % r], local_sem=S.left1,
                      pid=where[k][1], routing_id=where[k][0], dma_engine_mask=masks[k])
-    left1 = sum(lanes)
+    left1 = 4 * _bits(home) + sum(lanes[k] for k in NEAR)
+
+    giver = plans[behind[FAR]]["relay"]
+    ten.wait_ge(S.cw, 2 * _bits(topo.mask(giver[RELAYED[0]], core)))
+    ten.wait_ge(S.cx, 2 * _bits(topo.mask(giver[RELAYED[1]], core)))
+    for i in range(2):
+        ten.matmul_mx(bank1(0, i)[:, 0:NC], T.rw1q[:, NC * i:NC * (i + 1)], T.rw1p[:, NC * i:NC * (i + 1)],
+                      T.rxq[:], T.rxp[:], False, True).then_inc(S["mz%d" % i], 1)
 
     syn.wait_ge(S.left1, left1)
     syn.dma_start(T.w2s[:], T.w2[:]).then_inc(S.ldw2, 16)
 
-    vec.wait_ge(S["pf%d" % behind[1]], lanes_of(behind[1], False))
-    vec.wait_ge(S.mma0, 1)
-    vec.wait_ge(S.mmb0, 1)
-    vec.tensor_tensor(T.acc[:, 0:PW:2], T.land[:, 0:PW:2], bank1(0, 0)[:, 0:NC], add).then_inc(S.ad1, 1)
-    vec.tensor_tensor(T.acc[:, 1:PW:2], T.land[:, 1:PW:2], bank1(0, 1)[:, 0:NC], add).then_inc(S.ad1, 1)
-    for k in (2, 3, 4):
-        vec.wait_ge(S["ad%d" % (k - 1)], 2 if k == 2 else 1)
-        vec.wait_ge(S["pf%d" % behind[k]], lanes_of(behind[k], False))
-        vec.tensor_tensor(T.acc[:], T.acc[:], T.land[:, PW * (k - 1):PW * k], add).then_inc(S["ad%d" % k], 1)
+    def landed1(k):
+        return _bits(topo.mask(T.cores[behind[k]], core))
 
-    vec.wait_ge(S.ad4, 1)
+    vec.wait_ge(S["pf%d" % behind[1]], landed1(1))
+    vec.wait_ge(S["pf%d" % behind[2]], landed1(2))
+    vec.tensor_tensor(T.acc[:], T.land[:, 0:PW], T.land[:, PW:2 * PW], add).then_inc(S.ad2, 1)
+    vec.wait_ge(S.ad2, 1)
+    vec.wait_ge(S["pf%d" % behind[3]], landed1(3))
+    vec.tensor_tensor(T.acc[:], T.acc[:], T.land[:, 2 * PW:3 * PW], add).then_inc(S.ad3, 1)
+    vec.wait_ge(S.ad3, 1)
+    vec.wait_ge(S.mz0, 1)
+    vec.tensor_tensor(T.acc[:, 0:PW:2], T.acc[:, 0:PW:2], bank1(0, 0)[:, 0:NC], add).then_inc(S.ad4, 1)
+    vec.wait_ge(S.mz1, 1)
+    vec.tensor_tensor(T.acc[:, 1:PW:2], T.acc[:, 1:PW:2], bank1(0, 1)[:, 0:NC], add).then_inc(S.ad4, 1)
+
+    vec.wait_ge(S.ad4, 2)
     vec.tensor_scalar(T.ht[:, 0:TW:2], T.acc[:], 0.0, CS, AluOpType.max, AluOpType.mult).then_inc(S.hdone, 1)
-    act.wait_ge(S.ad4, 1)
+    act.wait_ge(S.ad4, 2)
     act.activation(T.ht[:, 1:TW:2], T.acc[:], ActivationFunctionType.Relu, scale=-CS).then_inc(S.hdone, 1)
     vec.wait_ge(S.hdone, 2)
     vec.quantize_mx(T.hq[:], T.hp[:], T.ht[:]).then_inc(S.qh, 1)
     vec.wait_ge(S.ldw2, 16)
     vec.quantize_mx(T.w2q[:], T.w2p[:], T.w2s[:]).then_inc(S.qw2, 1)
 
+    hand_ids = [DstId(rid=hand[k][0], pnc=hand[k][1]) for k in RELAYED]
     g.wait_ge(S.qh, 1)
     g.remote_dma_fused([RemoteDMATransfer(
-        dst_ids=[DstId(rid=where[k][0], pnc=where[k][1]) for k in range(1, N)], dma_engine_mask=common,
-        remote_sem=S["hf%d" % r], srcs=[T.hp[:]], dsts=[T.gp[:, NC * (k - 1):NC * k] for k in range(1, N)])],
+        dst_ids=hand_ids, dma_engine_mask=mine["hand"], remote_sem=S.rs,
+        srcs=[T.hp[:]], dsts=[T.fp[:] for _ in RELAYED])], local_sem=S.left2)
+    g.remote_dma_fused([RemoteDMATransfer(
+        dst_ids=hand_ids, dma_engine_mask=mine["hand"], remote_sem=S.rc,
+        srcs=[T.hq[:].bitcast(u8)], dsts=[T.fq[:].bitcast(u8) for _ in RELAYED])], local_sem=S.left2)
+    g.remote_dma_fused([RemoteDMATransfer(
+        dst_ids=[DstId(rid=where[k][0], pnc=where[k][1]) for k in DIRECT], dma_engine_mask=mine["away"],
+        remote_sem=S["hf%d" % r], srcs=[T.hp[:]], dsts=[T.gp[:, NC * (k - 1):NC * k] for k in DIRECT])],
         local_sem=S.left2)
-    for k in range(1, N):
-        g.remote_dma(out_ap=T.gq[:, NC * (k - 1):NC * k].bitcast(dt.uint8), in_ap=T.hq[:].bitcast(dt.uint8),
+    for k in DIRECT:
+        g.remote_dma(out_ap=T.gq[:, NC * (k - 1):NC * k].bitcast(u8), in_ap=T.hq[:].bitcast(u8),
                      remote_sem=S["hf%d" % r], local_sem=S.left2,
                      pid=where[k][1], routing_id=where[k][0], dma_engine_mask=masks[k])
-    left2 = lanes_common + sum(lanes)
+    left2 = 2 * _bits(mine["hand"]) + _bits(mine["away"]) + sum(lanes[k] for k in DIRECT)
+
+    def landed2(k):
+        j = behind[k]
+        if k in DIRECT:
+            return _bits(plans[j]["away"]) + _bits(topo.mask(T.cores[j], core))
+        return 2 * _bits(topo.mask(plans[j]["relay"][k], core))
 
     ten.wait_ge(S.qh, 1)
     ten.wait_ge(S.qw2, 1)
     for k in range(N):
-        ten.wait_ge(S["cp%d" % ((2 + k) // 2 + 1)], 2)
+        ten.wait_ge(S["cp%d" % (k // 2 + 1)], 2)
         if k == 0:
             rhs, rhs_scale = T.hq[:], T.hp[:]
         else:
-            ten.wait_ge(S["hf%d" % behind[k]], lanes_of(behind[k], True) + lanes_of(behind[k], False))
+            ten.wait_ge(S["hf%d" % behind[k]], landed2(k))
             rhs, rhs_scale = T.gq[:, NC * (k - 1):NC * k], T.gp[:, NC * (k - 1):NC * k]
         ten.matmul_mx(bank2(k)[:, 0:NC], T.w2q[:], T.w2p[:], rhs, rhs_scale, True, True).then_inc(S["ym%d" % k], 1)
         j = behind[k]

from concourse.bass import DstId, RemoteDMATransfer
from concourse.mybir import dt, AluOpType, ActivationFunctionType

N = 5
WORLD = 256
NC = 128
TW = 4 * NC
PW = 2 * NC
CS = 0.01923
NEAR = (1, 2, 3)
FAR = 4
DIRECT = (1, 2)
RELAYED = (3, 4)
HAND_ALL = True

SCRATCH = {
    "xs": ("sbuf", [128, N * TW], "bfloat16"),
    "w1s": ("sbuf", [128, 2 * TW], "bfloat16"),
    "w2s": ("sbuf", [128, TW], "bfloat16"),
    "xq": ("sbuf", [128, N * NC], "float8_e4m3fn_x4"),
    "xp": ("sbuf", [128, N * NC], "uint8"),
    "w1q": ("sbuf", [128, 2 * NC], "float8_e4m3fn_x4"),
    "w1p": ("sbuf", [128, 2 * NC], "uint8"),
    "w2q": ("sbuf", [128, NC], "float8_e4m3fn_x4"),
    "w2p": ("sbuf", [128, NC], "uint8"),
    "fw1q": ("sbuf", [128, 2 * NC], "float8_e4m3fn_x4"),
    "fw1p": ("sbuf", [128, 2 * NC], "uint8"),
    "fxq": ("sbuf", [128, NC], "float8_e4m3fn_x4"),
    "fxp": ("sbuf", [128, NC], "uint8"),
    "fq": ("sbuf", [128, NC], "float8_e4m3fn_x4"),
    "fp": ("sbuf", [128, NC], "uint8"),
    "rw1q": ("sbuf", [128, 2 * NC], "float8_e4m3fn_x4"),
    "rw1p": ("sbuf", [128, 2 * NC], "uint8"),
    "rxq": ("sbuf", [128, NC], "float8_e4m3fn_x4"),
    "rxp": ("sbuf", [128, NC], "uint8"),
    "out1": ("sbuf", [128, 3 * PW], "float32"),
    "land": ("sbuf", [128, 3 * PW], "float32"),
    "acc": ("sbuf", [128, PW], "float32"),
    "ht": ("sbuf", [128, TW], "bfloat16"),
    "hq": ("sbuf", [128, NC], "float8_e4m3fn_x4"),
    "hp": ("sbuf", [128, NC], "uint8"),
    "gq": ("sbuf", [128, 4 * NC], "float8_e4m3fn_x4"),
    "gp": ("sbuf", [128, 4 * NC], "uint8"),
    "ys": ("sbuf", [128, N * NC], "float32"),
}
for _b in range(8):
    SCRATCH["ps%d" % _b] = ("psum", [128, 512], "float32")

SEMAPHORES = (
    ["ldw1", "ldw2", "qw1", "qw2", "left1", "left2", "hdone", "qh", "st",
     "r1s", "r1c", "rs", "rc",
     "cw", "cx", "mz0", "mz1", "ad2", "ad3", "ad4"]
    + ["ldx%d" % k for k in range(N)] + ["qx%d" % k for k in range(N)]
    + ["mma%d" % k for k in NEAR] + ["mmb%d" % k for k in NEAR] + ["cp%d" % k for k in NEAR]
    + ["pf%d" % j for j in range(N)]
    + ["hf%d" % j for j in range(N)]
    + ["ym%d" % k for k in range(N)] + ["yc%d" % k for k in range(N)]
)


def _bits(m):
    return bin(m).count("1")


def _plan(topo, T, j):
    rc = T.cores[j]
    others = [T.cores[c] for c in range(N) if c != j]
    free = [c for c in range(WORLD)
            if topo.host(c) == topo.host(rc) and topo.chip(c) == topo.chip(rc) and topo.die(c) != topo.die(rc)
            and T.rank_of(c) is None and all(topo.may_write(c, d) for d in others)]
    relay = {k: free[n] for n, k in enumerate(RELAYED)}
    away = topo.mask(rc, others[0])
    for d in others:
        away &= topo.mask(rc, d)
    home = topo.mask(rc, relay[RELAYED[0]])
    for k in RELAYED:
        home &= topo.mask(rc, relay[k])
    stay = home & ~away
    stay = stay if stay else home
    return {"relay": relay, "away": away, "home": stay, "hand": home if HAND_ALL else stay}


def _relay_program(g, core, T, topo, j, k, plan):
    S = T.sem
    u8 = dt.uint8

    def send(dst, out_ap, in_ap, sem):
        rid, pid = topo.addr(dst, core)
        g.remote_dma(out_ap=out_ap, in_ap=in_ap, remote_sem=sem, local_sem=S.left2, pid=pid, routing_id=rid,
                     dma_engine_mask=topo.mask(core, dst))
        return _bits(topo.mask(core, dst))

    far = T.cores[(j + FAR) % N]
    if k == RELAYED[0]:
        sp, sq, dp, dq, sem = T.fw1p, T.fw1q, T.rw1p, T.rw1q, S.cw
    else:
        sp, sq, dp, dq, sem = T.fxp, T.fxq, T.rxp, T.rxq, S.cx
    left = 0
    g.wait_ge(S.r1s, _bits(plan["home"]))
    left += send(far, dp[:], sp[:], sem)
    g.wait_ge(S.r1c, _bits(plan["home"]))
    left += send(far, dq[:].bitcast(u8), sq[:].bitcast(u8), sem)
    dst = T.cores[(j + k) % N]
    g.wait_ge(S.rs, _bits(plan["hand"]))
    left += send(dst, T.gp[:, NC * (k - 1):NC * k], T.fp[:], S["hf%d" % j])
    g.wait_ge(S.rc, _bits(plan["hand"]))
    left += send(dst, T.gq[:, NC * (k - 1):NC * k].bitcast(u8), T.fq[:].bitcast(u8), S["hf%d" % j])
    g.wait_ge(S.left2, left)


def rank_program(g, core, T, topo):
    r = T.rank_of(core)
    plans = [_plan(topo, T, j) for j in range(N)]
    if r is None:
        for j in range(N):
            for k in RELAYED:
                if plans[j]["relay"][k] == core:
                    _relay_program(g, core, T, topo, j, k, plans[j])
        return
    S = T.sem
    u8 = dt.uint8
    vec, ten, act, syn = g.vector, g.tensor, g.scalar, g.sync
    ahead = [(r + k) % N for k in range(N)]
    behind = [(r - k) % N for k in range(N)]
    add = AluOpType.add
    mine = plans[r]
    home = mine["home"]

    dest = [T.cores[c] for c in ahead]
    where = [None] + [topo.addr(dest[k], core) for k in range(1, N)]
    masks = [None] + [topo.mask(core, dest[k]) for k in range(1, N)]
    lanes = [0] + [_bits(masks[k]) for k in range(1, N)]
    hand = {k: topo.addr(mine["relay"][k], core) for k in RELAYED}

    def bank1(k, i):
        return T["ps%d" % (2 * (k - 1) + i if k else 6 + i)]

    def bank2(k):
        return T["ps%d" % k]

    def xcols(k):
        c = ahead[k]
        return NC * c, NC * (c + 1)

    def load_x(queue, k):
        c = ahead[k]
        queue.dma_start(T.xs[:, TW * c:TW * (c + 1)], T.x[:, TW * c:TW * (c + 1)]).then_inc(S["ldx%d" % k], 16)

    syn.dma_start(T.w1s[:], T.w1[:]).then_inc(S.ldw1, 16)
    load_x(act, FAR)
    load_x(syn, 1)
    load_x(act, 2)
    load_x(syn, 3)
    load_x(act, 0)

    def to_relay(k, out_ap, in_ap, sem):
        g.remote_dma(out_ap=out_ap, in_ap=in_ap, remote_sem=sem, local_sem=S.left1,
                     pid=hand[k][1], routing_id=hand[k][0], dma_engine_mask=home)

    ten.wait_ge(S.qw1, 1)
    for k in (FAR,) + NEAR + (0,):
        lo_x, hi_x = xcols(k)
        vec.wait_ge(S["ldx%d" % k], 16)
        vec.quantize_mx(T.xq[:, lo_x:hi_x], T.xp[:, lo_x:hi_x],
                        T.xs[:, 4 * lo_x:4 * hi_x]).then_inc(S["qx%d" % k], 1)
        if k == FAR:
            vec.wait_ge(S.ldw1, 16)
            vec.quantize_mx(T.w1q[:], T.w1p[:], T.w1s[:]).then_inc(S.qw1, 1)
            g.wait_ge(S["qx%d" % k], 1)
            to_relay(RELAYED[1], T.fxp[:], T.xp[:, lo_x:hi_x], S.r1s)
            g.wait_ge(S.qw1, 1)
            to_relay(RELAYED[0], T.fw1p[:], T.w1p[:], S.r1s)
            to_relay(RELAYED[0], T.fw1q[:].bitcast(u8), T.w1q[:].bitcast(u8), S.r1c)
            to_relay(RELAYED[1], T.fxq[:].bitcast(u8), T.xq[:, lo_x:hi_x].bitcast(u8), S.r1c)
            continue
        ten.wait_ge(S["qx%d" % k], 1)
        for i, name in ((0, "mma%d"), (1, "mmb%d")):
            mm = ten.matmul_mx(bank1(k, i)[:, 0:NC], T.w1q[:, NC * i:NC * (i + 1)], T.w1p[:, NC * i:NC * (i + 1)],
                               T.xq[:, lo_x:hi_x], T.xp[:, lo_x:hi_x], True, k != 0)
            if k:
                mm.then_inc(S[name % k], 1)
        if k == 0:
            continue
        lo, hi = PW * (k - 1), PW * k
        vec.wait_ge(S["mma%d" % k], 1)
        vec.tensor_copy(T.out1[:, lo:hi:2], bank1(k, 0)[:, 0:NC]).then_inc(S["cp%d" % k], 1)
        act.wait_ge(S["mmb%d" % k], 1)
        act.activation(T.out1[:, lo + 1:hi:2], bank1(k, 1)[:, 0:NC], ActivationFunctionType.Copy).then_inc(S["cp%d" % k], 1)
        g.wait_ge(S["cp%d" % k], 2)
        g.remote_dma(out_ap=T.land[:, lo:hi], in_ap=T.out1[:, lo:hi], remote_sem=S["pf%d" % r], local_sem=S.left1,
                     pid=where[k][1], routing_id=where[k][0], dma_engine_mask=masks[k])
    left1 = 4 * _bits(home) + sum(lanes[k] for k in NEAR)

    giver = plans[behind[FAR]]["relay"]
    ten.wait_ge(S.cw, 2 * _bits(topo.mask(giver[RELAYED[0]], core)))
    ten.wait_ge(S.cx, 2 * _bits(topo.mask(giver[RELAYED[1]], core)))
    for i in range(2):
        ten.matmul_mx(bank1(0, i)[:, 0:NC], T.rw1q[:, NC * i:NC * (i + 1)], T.rw1p[:, NC * i:NC * (i + 1)],
                      T.rxq[:], T.rxp[:], False, True).then_inc(S["mz%d" % i], 1)

    syn.wait_ge(S.left1, left1)
    syn.dma_start(T.w2s[:], T.w2[:]).then_inc(S.ldw2, 16)

    def landed1(k):
        return _bits(topo.mask(T.cores[behind[k]], core))

    vec.wait_ge(S["pf%d" % behind[1]], landed1(1))
    vec.wait_ge(S["pf%d" % behind[2]], landed1(2))
    vec.tensor_tensor(T.acc[:], T.land[:, 0:PW], T.land[:, PW:2 * PW], add).then_inc(S.ad2, 1)
    vec.wait_ge(S.ad2, 1)
    vec.wait_ge(S["pf%d" % behind[3]], landed1(3))
    vec.tensor_tensor(T.acc[:], T.acc[:], T.land[:, 2 * PW:3 * PW], add).then_inc(S.ad3, 1)
    vec.wait_ge(S.ad3, 1)
    vec.wait_ge(S.mz0, 1)
    vec.tensor_tensor(T.acc[:, 0:PW:2], T.acc[:, 0:PW:2], bank1(0, 0)[:, 0:NC], add).then_inc(S.ad4, 1)
    vec.wait_ge(S.mz1, 1)
    vec.tensor_tensor(T.acc[:, 1:PW:2], T.acc[:, 1:PW:2], bank1(0, 1)[:, 0:NC], add).then_inc(S.ad4, 1)

    vec.wait_ge(S.ad4, 2)
    vec.tensor_scalar(T.ht[:, 0:TW:2], T.acc[:], 0.0, CS, AluOpType.max, AluOpType.mult).then_inc(S.hdone, 1)
    act.wait_ge(S.ad4, 2)
    act.activation(T.ht[:, 1:TW:2], T.acc[:], ActivationFunctionType.Relu, scale=-CS).then_inc(S.hdone, 1)
    vec.wait_ge(S.hdone, 2)
    vec.quantize_mx(T.hq[:], T.hp[:], T.ht[:]).then_inc(S.qh, 1)
    vec.wait_ge(S.ldw2, 16)
    vec.quantize_mx(T.w2q[:], T.w2p[:], T.w2s[:]).then_inc(S.qw2, 1)

    hand_ids = [DstId(rid=hand[k][0], pnc=hand[k][1]) for k in RELAYED]
    g.wait_ge(S.qh, 1)
    g.remote_dma_fused([RemoteDMATransfer(
        dst_ids=hand_ids, dma_engine_mask=mine["hand"], remote_sem=S.rs,
        srcs=[T.hp[:]], dsts=[T.fp[:] for _ in RELAYED])], local_sem=S.left2)
    g.remote_dma_fused([RemoteDMATransfer(
        dst_ids=hand_ids, dma_engine_mask=mine["hand"], remote_sem=S.rc,
        srcs=[T.hq[:].bitcast(u8)], dsts=[T.fq[:].bitcast(u8) for _ in RELAYED])], local_sem=S.left2)
    g.remote_dma_fused([RemoteDMATransfer(
        dst_ids=[DstId(rid=where[k][0], pnc=where[k][1]) for k in DIRECT], dma_engine_mask=mine["away"],
        remote_sem=S["hf%d" % r], srcs=[T.hp[:]], dsts=[T.gp[:, NC * (k - 1):NC * k] for k in DIRECT])],
        local_sem=S.left2)
    for k in DIRECT:
        g.remote_dma(out_ap=T.gq[:, NC * (k - 1):NC * k].bitcast(u8), in_ap=T.hq[:].bitcast(u8),
                     remote_sem=S["hf%d" % r], local_sem=S.left2,
                     pid=where[k][1], routing_id=where[k][0], dma_engine_mask=masks[k])
    left2 = 2 * _bits(mine["hand"]) + _bits(mine["away"]) + sum(lanes[k] for k in DIRECT)

    def landed2(k):
        j = behind[k]
        if k in DIRECT:
            return _bits(plans[j]["away"]) + _bits(topo.mask(T.cores[j], core))
        return 2 * _bits(topo.mask(plans[j]["relay"][k], core))

    ten.wait_ge(S.qh, 1)
    ten.wait_ge(S.qw2, 1)
    for k in range(N):
        ten.wait_ge(S["cp%d" % (k // 2 + 1)], 2)
        if k == 0:
            rhs, rhs_scale = T.hq[:], T.hp[:]
        else:
            ten.wait_ge(S["hf%d" % behind[k]], landed2(k))
            rhs, rhs_scale = T.gq[:, NC * (k - 1):NC * k], T.gp[:, NC * (k - 1):NC * k]
        ten.matmul_mx(bank2(k)[:, 0:NC], T.w2q[:], T.w2p[:], rhs, rhs_scale, True, True).then_inc(S["ym%d" % k], 1)
        j = behind[k]
        vec.wait_ge(S["ym%d" % k], 1)
        vec.tensor_copy(T.ys[:, NC * j:NC * (j + 1)], bank2(k)[:, 0:NC]).then_inc(S["yc%d" % k], 1)

    def store_y(queue, k):
        j = behind[k]
        queue.wait_ge(S["yc%d" % k], 1)
        queue.dma_start(T.y[:, NC * j:NC * (j + 1)], T.ys[:, NC * j:NC * (j + 1)]).then_inc(S.st, 16)

    syn.wait_ge(S.hdone, 2)
    syn.wait_ge(S.left2, left2)
    act.wait_ge(S.left2, left2)
    syn.dma_start(T.h[:], T.ht[:]).then_inc(S.st, 16)
    store_y(act, 0)
    store_y(syn, 1)
    store_y(act, 2)
    store_y(syn, 3)
    store_y(act, 4)

    g.wait_ge(S.left1, left1)
    g.wait_ge(S.left2, left2)
    g.wait_ge(S.st, 16 * (N + 1))
